import numpy as np
import ml_dtypes


def mxq(x, axis, fmt="e4m3"):
    dtype, down = {"e4m3": (ml_dtypes.float8_e4m3fn, 7), "e5m2": (ml_dtypes.float8_e5m2, 14)}[fmt]
    v = np.moveaxis(np.asarray(x, np.float32).astype(ml_dtypes.bfloat16).astype(np.float64), axis, -1)
    blocks = v.reshape(v.shape[:-1] + (-1, 32))
    amax = np.abs(blocks).max(-1, keepdims=True)
    byte = np.maximum(np.where(amax > 0, np.frexp(amax)[1] - 1 + 127, 0) - down, 1)
    scale = np.exp2(byte - 127.0)
    codes = (blocks / scale).astype(np.float32).astype(dtype).astype(np.float64)
    return np.moveaxis((codes * scale).reshape(v.shape), -1, axis)


WIDE = False


def mx_kscale(k):
    if not WIDE:
        return np.ones(k)
    levels = np.array([10, -10, 5, -5, 0])
    if k % 512:
        return np.exp2(np.random.permutation(np.resize(levels, k // 32))).repeat(32)
    a = np.empty((k // 512, 16))
    for p in range(k // 512):
        a[p, :8] = np.random.permutation(np.resize(levels, 8))
        for g in range(8):
            far = levels[np.abs(levels - a[p, g]) >= 10]
            a[p, g + 8] = far[np.random.randint(len(far))]
    return np.exp2(a.ravel()).repeat(32)


def f64(x):
    return np.asarray(x).astype(np.float64)


def striped(idx):
    return np.tile(idx.reshape(-1, 16).T, (8, 1)).astype(np.uint16)


def unstriped(offs):
    return offs[:16].T.reshape(-1).astype(np.int64)


def pack_weight(w):
    k, n = w.shape
    w = f64(np.asarray(w, np.float32).astype(ml_dtypes.bfloat16)).reshape(k // 32, 32, n)
    amax = np.abs(w).max(1)
    byte = np.clip(np.where(amax > 0, np.frexp(amax)[1] - 1 + 127 - 7, 1), 1, 254)
    scaled = (w * np.exp2(127.0 - byte)[:, None, :]).reshape(k, n).astype(np.float32)
    words = np.ascontiguousarray(scaled.reshape(k // 512, 128, 4, n).transpose(0, 1, 3, 2)).astype(ml_dtypes.float8_e4m3fn).view(np.uint8)
    return words, np.ascontiguousarray(byte.astype(np.uint8).reshape(k // 512, 16, n))


def unpack_weight(words, scales):
    g, p, n, _ = words.shape
    vals = np.ascontiguousarray(words).view(ml_dtypes.float8_e4m3fn).astype(np.float64) * np.repeat(np.exp2(scales.astype(np.float64) - 127.0), 8, axis=1)[..., None]
    return vals.transpose(0, 1, 3, 2).reshape(g * 512, n)


K, T, S, D, H, V, Z, W = 512, 2048, 512, 2, 512, 256, 512, 2048
P = 2 ** 7


def setup_inputs():
    n = np.random.standard_normal
    s = mx_kscale(K)[:, None]
    packed_xT = pack_weight(n((K, T)) * s)
    packed_eT = pack_weight(n((K, W)) * s)
    return {
        "x_words": packed_xT[0],
        "x_scales": packed_xT[1],
        "w1": (n((K, H)) / np.sqrt(K) / s).astype(np.float32),
        "e_words": packed_eT[0],
        "e_scales": packed_eT[1],
        "unit": (np.random.uniform(0.6, 1.4, (K, 1)) / np.sqrt(K) / s).astype(np.float32),
        "wgt": (np.tile(np.random.uniform(0.4, 1.6, W), (P, 1))).astype(np.float32),
        "offs": striped(np.random.permutation(T)[:S]),
        "plc": striped(np.random.permutation(W)[:Z]),
        "seq": striped(np.random.permutation(V)),
    }


def reference(x_words, x_scales, w1, e_words, e_scales, unit, wgt, offs, plc, seq):
    xq = unpack_weight(x_words, x_scales)[:, unstriped(offs)]
    y = mxq(f64(w1), 0, "e4m3").T @ xq
    y2 = (y) ** 2
    ms = y2.mean(axis=1, keepdims=True)
    nd = y / np.sqrt(ms + 0.1)
    sq_ = nd * np.abs(nd)
    agg = sq_.reshape(len(sq_), -1, D).sum(axis=2)
    smo = 0.6 * agg + 0.4 * agg[:, unstriped(seq)]
    hid = f64(unit) * smo
    e_plc = unpack_weight(e_words, e_scales)[:, unstriped(plc)]
    sc = mxq(hid, 0, "e4m3").T @ e_plc
    mu = sc.mean(axis=1, keepdims=True)
    best = sc.max(axis=1, keepdims=True)
    conf = (sc - mu) / (best - mu + 0.3)
    return conf * (f64(wgt)[:1][:, unstriped(plc)])

@@ -1,0 +1,177 @@
+from contextlib import ExitStack
+
+import concourse.mybir as mybir
+
+K, T, S, H, V, Z, W = 512, 2048, 512, 512, 256, 512, 2048
+FLOPS = 2 * K * H * S + 2 * H * V * Z
+
+F32 = mybir.dt.float32
+BF16 = mybir.dt.bfloat16
+I32 = mybir.dt.int32
+U32 = mybir.dt.uint32
+U16 = mybir.dt.uint16
+U8 = mybir.dt.uint8
+FP8X4 = mybir.dt.float8_e4m3fn_x4
+ALU = mybir.AluOpType
+ACT = mybir.ActivationFunctionType
+AX = mybir.AxisListType
+
+P = 128
+PACK = 4
+HALVES = V // P
+
+
+def tile_picked_yplacer_conf_p_kernel(
+    tc, x_words, x_scales, w1, e_words, e_scales, unit, wgt, offs, plc, seq, out
+):
+    nc = tc.nc
+    with ExitStack() as ctx:
+        keep = ctx.enter_context(tc.tile_pool(name="keep", bufs=1))
+        psum = ctx.enter_context(tc.psum_pool(name="psum", bufs=1))
+
+        offs_sb = keep.tile([P, S // 16], U16, name="offs_sb")
+        plc_sb = keep.tile([P, Z // 16], U16, name="plc_sb")
+        seq_sb = keep.tile([P, V // 16], U16, name="seq_sb")
+        x_table = keep.tile([P, T], U32, name="x_table", tag="x_then_wgt")
+        x_scale_table = keep.tile([P, T], U8, name="x_scale_table")
+        e_table = keep.tile([P, W], U32, name="e_table")
+        e_scale_table = keep.tile([P, W], U8, name="e_scale_table")
+        w_raw = [keep.tile([P, PACK, H // 2], F32, name=f"w_raw{c}") for c in range(2)]
+        unit_sb = keep.tile([P, PACK], F32, name="unit_sb")
+
+        nc.gpsimd.memset(x_scale_table[:].bitcast(I32), 0)
+        nc.gpsimd.memset(e_scale_table[:].bitcast(I32), 0)
+
+        nc.sync.dma_start(offs_sb[:], offs)
+        nc.sync.dma_start(plc_sb[:], plc)
+        nc.sync.dma_start(seq_sb[:], seq)
+        for q in range(4):
+            nc.scalar.dma_start(
+                x_scale_table[32 * q : 32 * q + 4, :].bitcast(I32),
+                x_scales[0, 4 * q : 4 * q + 4, :].bitcast(I32),
+            )
+        nc.sync.dma_start(x_table[:].bitcast(I32), x_words[0].rearrange("p n r -> p (n r)").bitcast(I32))
+        w_rows = w1.rearrange("(p j) c -> p j c", j=PACK)
+        for c in range(2):
+            nc.sync.dma_start(w_raw[c][:], w_rows[:, :, c * (H // 2) : (c + 1) * (H // 2)])
+        nc.gpsimd.dma_start(unit_sb[:], unit.rearrange("(p t) o -> p (t o)", t=PACK))
+        for q in range(4):
+            nc.gpsimd.dma_start(
+                e_scale_table[32 * q : 32 * q + 4, :].bitcast(I32),
+                e_scales[0, 4 * q : 4 * q + 4, :].bitcast(I32),
+            )
+        nc.sync.dma_start(e_table[:].bitcast(I32), e_words[0].rearrange("p n r -> p (n r)").bitcast(I32))
+
+        x_codes = keep.tile([P, S], U32, name="x_codes", align_bytes=64)
+        x_planes = keep.tile([P, S], U8, name="x_planes", align_bytes=64)
+        e_codes = keep.tile([P, Z], U32, name="e_codes", align_bytes=64)
+        nc.vector.tensor_copy(x_planes[:], x_scale_table[:].indirect(offs_sb[:]))
+        nc.vector.tensor_copy(x_codes[:], x_table[:].indirect(offs_sb[:]))
+        wgt_table = keep.tile([P, W], F32, name="wgt_table", tag="x_then_wgt")
+        nc.sync.dma_start(wgt_table[:], wgt)
+
+        w_bf = keep.tile([P, PACK * H], BF16, name="w_bf", align_bytes=64, tag="w_then_e_planes")
+        w_dealt = w_bf[:].rearrange("p (t m j) -> p m j t", t=PACK, j=PACK)
+        m_half = P // 2
+        nc.scalar.copy(w_dealt[:, 0:m_half], w_raw[0][:].rearrange("p j (m t) -> p m j t", t=PACK))
+        m_cut = 44
+        src1 = w_raw[1][:].rearrange("p j (m t) -> p m j t", t=PACK)
+        nc.vector.tensor_copy(w_dealt[:, m_half : m_half + m_cut], src1[:, 0:m_cut])
+        nc.scalar.copy(w_dealt[:, m_half + m_cut : P], src1[:, m_cut:m_half])
+
+        w_codes = keep.tile([P, H], U32, name="w_codes", align_bytes=64)
+        w_planes = keep.tile([P, H], U8, name="w_planes", align_bytes=64)
+        y = [psum.tile([P, S], F32, name=f"y{t}") for t in range(PACK)]
+        for t in range(PACK):
+            cols = slice(t * P, (t + 1) * P)
+            nc.vector.quantize_mx(
+                out=w_codes[:, cols].bitcast(FP8X4),
+                scales=w_planes[:, cols],
+                in_=w_bf[:, t * PACK * P : (t + 1) * PACK * P],
+            )
+            nc.tensor.matmul_mx(
+                out=y[t][:],
+                lhsT=w_codes[:, cols].bitcast(FP8X4),
+                lhsT_scale=w_planes[:, cols],
+                rhs=x_codes[:].bitcast(FP8X4),
+                rhs_scale=x_planes[:],
+                start=True,
+                stop=True,
+            )
+
+        half_sign = keep.tile([P, PACK], F32, name="half_sign")
+        nc.vector.tensor_scalar(half_sign[:], unit_sb[:], 0.0, 0.5, ALU.is_ge, ALU.subtract)
+        slope = keep.tile([P, PACK], F32, name="slope")
+        nc.vector.tensor_scalar(slope[:], half_sign[:], 2.0 / (0.6 * S), None, ALU.mult)
+
+        e_planes = keep.tile([P, Z], U8, name="e_planes", align_bytes=64, tag="w_then_e_planes")
+        nc.vector.tensor_copy(e_planes[:], e_scale_table[:].indirect(plc_sb[:]))
+        nc.vector.tensor_copy(e_codes[:], e_table[:].indirect(plc_sb[:]))
+
+        agg = keep.tile([P, PACK * V], F32, name="agg")
+        fetched = [keep.tile([P, PACK * P], F32, name=f"fetched{h}") for h in range(HALVES)]
+        for t in range(PACK):
+            squares = keep.tile([P, S], F32, name="squares")
+            ssq = keep.tile([P, 1], F32, name=f"ssq{t}")
+            nc.scalar.activation(squares[:], y[t][:], ACT.Square, accum_out=ssq[:])
+            mag = keep.tile([P, S], F32, name=f"mag{t}")
+            nc.scalar.activation(mag[:], y[t][:], ACT.Abs, scale=unit_sb[:, t : t + 1])
+            den = keep.tile([P, 1], F32, name=f"den{t}")
+            nc.vector.tensor_scalar(den[:], ssq[:], 0.1 * S, slope[:, t : t + 1], ALU.add, ALU.mult)
+            gain = keep.tile([P, 1], F32, name=f"gain{t}")
+            nc.vector.reciprocal(gain[:], den[:])
+            signed = keep.tile([P, V, 2], F32, name=f"signed{t}", tag=f"signed{t}")
+            nc.vector.scalar_tensor_tensor(
+                signed[:].rearrange("p v d -> p (v d)"), y[t][:], gain[:], mag[:], ALU.mult, ALU.mult
+            )
+            nc.vector.tensor_tensor(agg[:, t * V : (t + 1) * V], signed[:, :, 0], signed[:, :, 1], ALU.add)
+        for t in range(PACK):
+            for h in range(HALVES):
+                nc.scalar.activation(
+                    fetched[h][:, t * P : (t + 1) * P],
+                    agg[:, t * V : (t + 1) * V].indirect(seq_sb[:, h * (P // 16) : (h + 1) * (P // 16)]),
+                    ACT.Copy,
+                    scale=0.4 / 0.6,
+                )
+
+        place_wgt = keep.tile([P, Z], F32, name="place_wgt", tag=f"signed{PACK - 1}")
+        nc.scalar.activation(place_wgt[:], wgt_table[:].indirect(plc_sb[:]), ACT.Copy)
+
+        sc = [psum.tile([P, Z], F32, name=f"sc{h}") for h in range(HALVES)]
+        own = agg[:].rearrange("p (t v) -> p t v", t=PACK)
+        for h in range(HALVES):
+            hid = keep.tile([P, PACK * P], BF16, name=f"hid{h}", align_bytes=64)
+            nc.vector.tensor_tensor(
+                hid[:].rearrange("p (c i t) -> p c t i", i=4, t=PACK),
+                own[:, :, h * P : (h + 1) * P].rearrange("p t (c i) -> p c t i", i=4),
+                fetched[h][:].rearrange("p (t c i) -> p c t i", i=4, t=PACK),
+                ALU.add,
+            )
+            hid_codes = keep.tile([P, P], U32, name=f"hid_codes{h}", align_bytes=64)
+            hid_planes = keep.tile([P, P], U8, name=f"hid_planes{h}", align_bytes=64)
+            nc.vector.quantize_mx(out=hid_codes[:].bitcast(FP8X4), scales=hid_planes[:], in_=hid[:])
+            nc.tensor.matmul_mx(
+                out=sc[h][:],
+                lhsT=hid_codes[:].bitcast(FP8X4),
+                lhsT_scale=hid_planes[:],
+                rhs=e_codes[:].bitcast(FP8X4),
+                rhs_scale=e_planes[:],
+                start=True,
+                stop=True,
+            )
+
+        for h in range(HALVES):
+            shares = keep.tile([P, Z], F32, name="shares")
+            mu = keep.tile([P, 1], F32, name=f"mu{h}")
+            nc.scalar.activation(shares[:], sc[h][:], ACT.Copy, scale=1.0 / Z, accum_out=mu[:])
+            best = keep.tile([P, 1], F32, name=f"best{h}")
+            nc.vector.tensor_reduce(best[:], sc[h][:], AX.X, ALU.max)
+            spread = keep.tile([P, 1], F32, name=f"spread{h}")
+            nc.vector.tensor_scalar(spread[:], best[:], mu[:], 0.3, ALU.subtract, ALU.add)
+            centred = keep.tile([P, Z], F32, name=f"centred{h}")
+            nc.vector.scalar_tensor_tensor(centred[:], sc[h][:], mu[:], place_wgt[:], ALU.subtract, ALU.mult)
+            inv = keep.tile([P, 1], F32, name=f"inv{h}")
+            nc.vector.reciprocal(inv[:], spread[:])
+            res = keep.tile([P, Z], F32, name=f"res{h}")
+            nc.scalar.activation(res[:], centred[:], ACT.Copy, scale=inv[:])
+            nc.sync.dma_start(out[h * P : (h + 1) * P, :], res[:])

@@ -19,6 +19,8 @@ AX = mybir.AxisListType
 P = 128
 PACK = 4
 HALVES = V // P
+CAST_SPLIT = 36
+LAST_SPLIT = 192
 
 
 def tile_picked_yplacer_conf_p_kernel(
@@ -34,50 +36,46 @@ def tile_picked_yplacer_conf_p_kernel(
         seq_sb = keep.tile([P, V // 16], U16, name="seq_sb")
         x_table = keep.tile([P, T], U32, name="x_table", tag="x_then_wgt")
         x_scale_table = keep.tile([P, T], U8, name="x_scale_table")
-        e_table = keep.tile([P, W], U32, name="e_table")
         e_scale_table = keep.tile([P, W], U8, name="e_scale_table")
         w_raw = [keep.tile([P, PACK, H // 2], F32, name=f"w_raw{c}") for c in range(2)]
         unit_sb = keep.tile([P, PACK], F32, name="unit_sb")
+        e_table = keep.tile([P, W], U32, name="e_table")
+        e_planes = keep.tile([P, Z], U8, name="e_planes", align_bytes=64)
 
-        nc.gpsimd.memset(x_scale_table[:].bitcast(I32), 0)
+        nc.vector.memset(x_scale_table[:].bitcast(I32), 0)
         nc.gpsimd.memset(e_scale_table[:].bitcast(I32), 0)
+        nc.gpsimd.memset(e_planes[:].bitcast(I32), 0)
 
+        w_rows = w1.rearrange("(p j) c -> p j c", j=PACK)
         nc.sync.dma_start(offs_sb[:], offs)
         nc.sync.dma_start(plc_sb[:], plc)
-        nc.sync.dma_start(seq_sb[:], seq)
+        nc.sync.dma_start(w_raw[0][:], w_rows[:, :, 0 : H // 2])
         for q in range(4):
-            nc.scalar.dma_start(
+            nc.sync.dma_start(
                 x_scale_table[32 * q : 32 * q + 4, :].bitcast(I32),
                 x_scales[0, 4 * q : 4 * q + 4, :].bitcast(I32),
             )
         nc.sync.dma_start(x_table[:].bitcast(I32), x_words[0].rearrange("p n r -> p (n r)").bitcast(I32))
-        w_rows = w1.rearrange("(p j) c -> p j c", j=PACK)
-        for c in range(2):
-            nc.sync.dma_start(w_raw[c][:], w_rows[:, :, c * (H // 2) : (c + 1) * (H // 2)])
-        nc.gpsimd.dma_start(unit_sb[:], unit.rearrange("(p t) o -> p (t o)", t=PACK))
-        for q in range(4):
-            nc.gpsimd.dma_start(
-                e_scale_table[32 * q : 32 * q + 4, :].bitcast(I32),
-                e_scales[0, 4 * q : 4 * q + 4, :].bitcast(I32),
-            )
+        nc.sync.dma_start(w_raw[1][:], w_rows[:, :, H // 2 : H])
+        nc.sync.dma_start(e_scale_table[0:16, :].bitcast(I32), e_scales[0].bitcast(I32))
+        nc.sync.dma_start(unit_sb[:], unit.rearrange("(p t) o -> p (t o)", t=PACK))
+        nc.sync.dma_start(seq_sb[:], seq)
         nc.sync.dma_start(e_table[:].bitcast(I32), e_words[0].rearrange("p n r -> p (n r)").bitcast(I32))
 
-        x_codes = keep.tile([P, S], U32, name="x_codes", align_bytes=64)
         x_planes = keep.tile([P, S], U8, name="x_planes", align_bytes=64)
-        e_codes = keep.tile([P, Z], U32, name="e_codes", align_bytes=64)
         nc.vector.tensor_copy(x_planes[:], x_scale_table[:].indirect(offs_sb[:]))
+        x_codes = keep.tile([P, S], U32, name="x_codes", align_bytes=64)
         nc.vector.tensor_copy(x_codes[:], x_table[:].indirect(offs_sb[:]))
         wgt_table = keep.tile([P, W], F32, name="wgt_table", tag="x_then_wgt")
         nc.sync.dma_start(wgt_table[:], wgt)
 
-        w_bf = keep.tile([P, PACK * H], BF16, name="w_bf", align_bytes=64, tag="w_then_e_planes")
+        w_bf = keep.tile([P, PACK * H], BF16, name="w_bf", align_bytes=64, tag="w_then_e_rows")
         w_dealt = w_bf[:].rearrange("p (t m j) -> p m j t", t=PACK, j=PACK)
+        w_src = [w_raw[c][:].rearrange("p j (m t) -> p m j t", t=PACK) for c in range(2)]
         m_half = P // 2
-        nc.scalar.copy(w_dealt[:, 0:m_half], w_raw[0][:].rearrange("p j (m t) -> p m j t", t=PACK))
-        m_cut = 44
-        src1 = w_raw[1][:].rearrange("p j (m t) -> p m j t", t=PACK)
-        nc.vector.tensor_copy(w_dealt[:, m_half : m_half + m_cut], src1[:, 0:m_cut])
-        nc.scalar.copy(w_dealt[:, m_half + m_cut : P], src1[:, m_cut:m_half])
+        nc.scalar.copy(w_dealt[:, 0:m_half], w_src[0])
+        nc.vector.tensor_copy(w_dealt[:, m_half : m_half + CAST_SPLIT], w_src[1][:, 0:CAST_SPLIT])
+        nc.scalar.copy(w_dealt[:, m_half + CAST_SPLIT : P], w_src[1][:, CAST_SPLIT:m_half])
 
         w_codes = keep.tile([P, H], U32, name="w_codes", align_bytes=64)
         w_planes = keep.tile([P, H], U8, name="w_planes", align_bytes=64)
@@ -100,33 +98,43 @@ def tile_picked_yplacer_conf_p_kernel(
             )
 
         half_sign = keep.tile([P, PACK], F32, name="half_sign")
-        nc.vector.tensor_scalar(half_sign[:], unit_sb[:], 0.0, 0.5, ALU.is_ge, ALU.subtract)
+        nc.gpsimd.tensor_scalar(half_sign[:], unit_sb[:], 0.0, 0.5, ALU.is_ge, ALU.subtract)
         slope = keep.tile([P, PACK], F32, name="slope")
-        nc.vector.tensor_scalar(slope[:], half_sign[:], 2.0 / (0.6 * S), None, ALU.mult)
+        nc.gpsimd.tensor_scalar(slope[:], half_sign[:], 2.0 / (0.6 * S), 0.0, ALU.mult, ALU.add)
 
-        e_planes = keep.tile([P, Z], U8, name="e_planes", align_bytes=64, tag="w_then_e_planes")
-        nc.vector.tensor_copy(e_planes[:], e_scale_table[:].indirect(plc_sb[:]))
-        nc.vector.tensor_copy(e_codes[:], e_table[:].indirect(plc_sb[:]))
+        e_rows = keep.tile([P, Z], U8, name="e_rows", tag="w_then_e_rows", align_bytes=64)
+        nc.vector.tensor_copy(e_rows[:], e_scale_table[:].indirect(plc_sb[:]))
+        for q in range(4):
+            nc.sync.dma_start(
+                e_planes[32 * q : 32 * q + 4, :].bitcast(I32), e_rows[4 * q : 4 * q + 4, :].bitcast(I32)
+            )
 
         agg = keep.tile([P, PACK * V], F32, name="agg")
-        fetched = [keep.tile([P, PACK * P], F32, name=f"fetched{h}") for h in range(HALVES)]
-        for t in range(PACK):
-            squares = keep.tile([P, S], F32, name="squares")
-            ssq = keep.tile([P, 1], F32, name=f"ssq{t}")
-            nc.scalar.activation(squares[:], y[t][:], ACT.Square, accum_out=ssq[:])
-            mag = keep.tile([P, S], F32, name=f"mag{t}")
-            nc.scalar.activation(mag[:], y[t][:], ACT.Abs, scale=unit_sb[:, t : t + 1])
-            den = keep.tile([P, 1], F32, name=f"den{t}")
-            nc.vector.tensor_scalar(den[:], ssq[:], 0.1 * S, slope[:, t : t + 1], ALU.add, ALU.mult)
-            gain = keep.tile([P, 1], F32, name=f"gain{t}")
+        fetched = [keep.tile([P, PACK * P], F32, name=f"fetched{h}", tag=f"fetched{h}") for h in range(HALVES)]
+        for t0 in range(0, PACK, 2):
+            ssq = keep.tile([P, 2], F32, name=f"ssq{t0}")
+            for u in range(2):
+                squares = keep.tile([P, S], F32, name="squares")
+                nc.scalar.activation(squares[:], y[t0 + u][:], ACT.Square, accum_out=ssq[:, u : u + 1])
+            den = keep.tile([P, 2], F32, name=f"den{t0}")
+            nc.vector.scalar_tensor_tensor(den[:], ssq[:], 0.1 * S, slope[:, t0 : t0 + 2], ALU.add, ALU.mult)
+            gain = keep.tile([P, 2], F32, name=f"gain{t0}")
             nc.vector.reciprocal(gain[:], den[:])
-            signed = keep.tile([P, V, 2], F32, name=f"signed{t}", tag=f"signed{t}")
-            nc.vector.scalar_tensor_tensor(
-                signed[:].rearrange("p v d -> p (v d)"), y[t][:], gain[:], mag[:], ALU.mult, ALU.mult
-            )
-            nc.vector.tensor_tensor(agg[:, t * V : (t + 1) * V], signed[:, :, 0], signed[:, :, 1], ALU.add)
-        for t in range(PACK):
-            for h in range(HALVES):
+            signed = []
+            for u in range(2):
+                t = t0 + u
+                mag = keep.tile([P, S], F32, name=f"mag{t}")
+                nc.scalar.activation(mag[:], y[t][:], ACT.Abs, scale=unit_sb[:, t : t + 1])
+                sg = keep.tile([P, V, 2], F32, name=f"signed{t}", tag=f"signed{t}", align_bytes=64)
+                nc.vector.scalar_tensor_tensor(
+                    sg[:].rearrange("p v d -> p (v d)"), y[t][:], gain[:, u : u + 1], mag[:], ALU.mult, ALU.mult
+                )
+                signed.append(sg)
+            for u in range(2):
+                t = t0 + u
+                nc.vector.tensor_tensor(agg[:, t * V : (t + 1) * V], signed[u][:, :, 0], signed[u][:, :, 1], ALU.add)
+        for h in range(HALVES):
+            for t in range(PACK):
                 nc.scalar.activation(
                     fetched[h][:, t * P : (t + 1) * P],
                     agg[:, t * V : (t + 1) * V].indirect(seq_sb[:, h * (P // 16) : (h + 1) * (P // 16)]),
@@ -134,13 +142,13 @@ def tile_picked_yplacer_conf_p_kernel(
                     scale=0.4 / 0.6,
                 )
 
-        place_wgt = keep.tile([P, Z], F32, name="place_wgt", tag=f"signed{PACK - 1}")
-        nc.scalar.activation(place_wgt[:], wgt_table[:].indirect(plc_sb[:]), ACT.Copy)
+        e_codes = keep.tile([P, Z], U32, name="e_codes", tag=f"signed{PACK - 1}", align_bytes=64)
+        nc.vector.tensor_copy(e_codes[:], e_table[:].indirect(plc_sb[:]))
 
         sc = [psum.tile([P, Z], F32, name=f"sc{h}") for h in range(HALVES)]
         own = agg[:].rearrange("p (t v) -> p t v", t=PACK)
         for h in range(HALVES):
-            hid = keep.tile([P, PACK * P], BF16, name=f"hid{h}", align_bytes=64)
+            hid = keep.tile([P, PACK * P], BF16, name=f"hid{h}", tag=f"hid{h}", align_bytes=64)
             nc.vector.tensor_tensor(
                 hid[:].rearrange("p (c i t) -> p c t i", i=4, t=PACK),
                 own[:, :, h * P : (h + 1) * P].rearrange("p t (c i) -> p c t i", i=4),
@@ -160,18 +168,31 @@ def tile_picked_yplacer_conf_p_kernel(
                 stop=True,
             )
 
+        place_wgt = keep.tile([P, Z], F32, name="place_wgt", tag="fetched0")
+        nc.scalar.activation(place_wgt[:], wgt_table[:].indirect(plc_sb[:]), ACT.Copy)
+
+        best = [keep.tile([P, 1], F32, name=f"best{h}") for h in range(HALVES)]
+        mu = [keep.tile([P, 1], F32, name=f"mu{h}") for h in range(HALVES)]
         for h in range(HALVES):
+            nc.vector.tensor_reduce(best[h][:], sc[h][:], AX.X, ALU.max)
             shares = keep.tile([P, Z], F32, name="shares")
-            mu = keep.tile([P, 1], F32, name=f"mu{h}")
-            nc.scalar.activation(shares[:], sc[h][:], ACT.Copy, scale=1.0 / Z, accum_out=mu[:])
-            best = keep.tile([P, 1], F32, name=f"best{h}")
-            nc.vector.tensor_reduce(best[:], sc[h][:], AX.X, ALU.max)
+            nc.scalar.activation(shares[:], sc[h][:], ACT.Copy, scale=1.0 / Z, accum_out=mu[h][:])
+        for h in range(HALVES):
             spread = keep.tile([P, 1], F32, name=f"spread{h}")
-            nc.vector.tensor_scalar(spread[:], best[:], mu[:], 0.3, ALU.subtract, ALU.add)
+            nc.vector.tensor_scalar(spread[:], best[h][:], mu[h][:], 0.3, ALU.subtract, ALU.add)
             centred = keep.tile([P, Z], F32, name=f"centred{h}")
-            nc.vector.scalar_tensor_tensor(centred[:], sc[h][:], mu[:], place_wgt[:], ALU.subtract, ALU.mult)
+            nc.vector.scalar_tensor_tensor(centred[:], sc[h][:], mu[h][:], place_wgt[:], ALU.subtract, ALU.mult)
             inv = keep.tile([P, 1], F32, name=f"inv{h}")
             nc.vector.reciprocal(inv[:], spread[:])
-            res = keep.tile([P, Z], F32, name=f"res{h}")
-            nc.scalar.activation(res[:], centred[:], ACT.Copy, scale=inv[:])
-            nc.sync.dma_start(out[h * P : (h + 1) * P, :], res[:])
+            rows = slice(h * P, (h + 1) * P)
+            if h == 0:
+                res = keep.tile([P, Z], F32, name="res")
+                nc.scalar.activation(res[:], centred[:], ACT.Copy, scale=inv[:])
+                nc.sync.dma_start(out[rows, :], res[:])
+            else:
+                left = keep.tile([P, LAST_SPLIT], F32, name="left")
+                right = keep.tile([P, Z - LAST_SPLIT], F32, name="right")
+                nc.scalar.activation(left[:], centred[:, 0:LAST_SPLIT], ACT.Copy, scale=inv[:])
+                nc.vector.tensor_scalar(right[:], centred[:, LAST_SPLIT:Z], inv[:], None, ALU.mult)
+                nc.scalar.dma_start(out[rows, 0:LAST_SPLIT], left[:])
+                nc.sync.dma_start(out[rows, LAST_SPLIT:Z], right[:])

@@ -111,6 +111,15 @@ def tile_picked_yplacer_conf_p_kernel(
 
         agg = keep.tile([P, PACK * V], F32, name="agg")
         fetched = [keep.tile([P, PACK * P], F32, name=f"fetched{h}", tag=f"fetched{h}") for h in range(HALVES)]
+        side = Z // 2
+        e_codes = []
+
+        def gather_places(b, tag):
+            codes = keep.tile([P, side], U32, name=f"e_codes{b}", tag=tag, align_bytes=64)
+            nc.vector.tensor_copy(codes[:], e_table[:].indirect(plc_sb[:, b * (side // 16) : (b + 1) * (side // 16)]))
+            e_codes.append(codes)
+
+        gather_places(0, "e_codes0")
         for t0 in range(0, PACK, 2):
             ssq = keep.tile([P, 2], F32, name=f"ssq{t0}")
             for u in range(2):
@@ -132,7 +141,8 @@ def tile_picked_yplacer_conf_p_kernel(
                 signed.append(sg)
             for u in range(2):
                 t = t0 + u
-                nc.vector.tensor_tensor(agg[:, t * V : (t + 1) * V], signed[u][:, :, 0], signed[u][:, :, 1], ALU.add)
+                adder = nc.gpsimd if t0 == 0 else nc.vector
+                adder.tensor_tensor(agg[:, t * V : (t + 1) * V], signed[u][:, :, 0], signed[u][:, :, 1], ALU.add)
         for h in range(HALVES):
             for t in range(PACK):
                 nc.scalar.activation(
@@ -142,8 +152,7 @@ def tile_picked_yplacer_conf_p_kernel(
                     scale=0.4 / 0.6,
                 )
 
-        e_codes = keep.tile([P, Z], U32, name="e_codes", tag=f"signed{PACK - 1}", align_bytes=64)
-        nc.vector.tensor_copy(e_codes[:], e_table[:].indirect(plc_sb[:]))
+        gather_places(1, f"signed{PACK - 1}")
 
         sc = [psum.tile([P, Z], F32, name=f"sc{h}") for h in range(HALVES)]
         own = agg[:].rearrange("p (t v) -> p t v", t=PACK)
@@ -158,15 +167,16 @@ def tile_picked_yplacer_conf_p_kernel(
             hid_codes = keep.tile([P, P], U32, name=f"hid_codes{h}", align_bytes=64)
             hid_planes = keep.tile([P, P], U8, name=f"hid_planes{h}", align_bytes=64)
             nc.vector.quantize_mx(out=hid_codes[:].bitcast(FP8X4), scales=hid_planes[:], in_=hid[:])
-            nc.tensor.matmul_mx(
-                out=sc[h][:],
-                lhsT=hid_codes[:].bitcast(FP8X4),
-                lhsT_scale=hid_planes[:],
-                rhs=e_codes[:].bitcast(FP8X4),
-                rhs_scale=e_planes[:],
-                start=True,
-                stop=True,
-            )
+            for b in range(2):
+                nc.tensor.matmul_mx(
+                    out=sc[h][:, b * side : (b + 1) * side],
+                    lhsT=hid_codes[:].bitcast(FP8X4),
+                    lhsT_scale=hid_planes[:],
+                    rhs=e_codes[b][:].bitcast(FP8X4),
+                    rhs_scale=e_planes[:, b * side : (b + 1) * side],
+                    start=True,
+                    stop=True,
+                )
 
         place_wgt = keep.tile([P, Z], F32, name="place_wgt", tag="fetched0")
         nc.scalar.activation(place_wgt[:], wgt_table[:].indirect(plc_sb[:]), ACT.Copy)

from contextlib import ExitStack

import concourse.mybir as mybir

K, T, S, H, V, Z, W = 512, 2048, 512, 512, 256, 512, 2048
FLOPS = 2 * K * H * S + 2 * H * V * Z

F32 = mybir.dt.float32
BF16 = mybir.dt.bfloat16
I32 = mybir.dt.int32
U32 = mybir.dt.uint32
U16 = mybir.dt.uint16
U8 = mybir.dt.uint8
FP8X4 = mybir.dt.float8_e4m3fn_x4
ALU = mybir.AluOpType
ACT = mybir.ActivationFunctionType
AX = mybir.AxisListType

P = 128
PACK = 4
HALVES = V // P
CAST_SPLIT = 36
LAST_SPLIT = 192


def tile_picked_yplacer_conf_p_kernel(
    tc, x_words, x_scales, w1, e_words, e_scales, unit, wgt, offs, plc, seq, out
):
    nc = tc.nc
    with ExitStack() as ctx:
        keep = ctx.enter_context(tc.tile_pool(name="keep", bufs=1))
        psum = ctx.enter_context(tc.psum_pool(name="psum", bufs=1))

        offs_sb = keep.tile([P, S // 16], U16, name="offs_sb")
        plc_sb = keep.tile([P, Z // 16], U16, name="plc_sb")
        seq_sb = keep.tile([P, V // 16], U16, name="seq_sb")
        x_table = keep.tile([P, T], U32, name="x_table", tag="x_then_wgt")
        x_scale_table = keep.tile([P, T], U8, name="x_scale_table")
        e_scale_table = keep.tile([P, W], U8, name="e_scale_table")
        w_raw = [keep.tile([P, PACK, H // 2], F32, name=f"w_raw{c}") for c in range(2)]
        unit_sb = keep.tile([P, PACK], F32, name="unit_sb")
        e_table = keep.tile([P, W], U32, name="e_table")
        e_planes = keep.tile([P, Z], U8, name="e_planes", align_bytes=64)

        nc.vector.memset(x_scale_table[:].bitcast(I32), 0)
        nc.gpsimd.memset(e_scale_table[:].bitcast(I32), 0)
        nc.gpsimd.memset(e_planes[:].bitcast(I32), 0)

        w_rows = w1.rearrange("(p j) c -> p j c", j=PACK)
        nc.sync.dma_start(offs_sb[:], offs)
        nc.sync.dma_start(plc_sb[:], plc)
        nc.sync.dma_start(w_raw[0][:], w_rows[:, :, 0 : H // 2])
        for q in range(4):
            nc.sync.dma_start(
                x_scale_table[32 * q : 32 * q + 4, :].bitcast(I32),
                x_scales[0, 4 * q : 4 * q + 4, :].bitcast(I32),
            )
        nc.sync.dma_start(x_table[:].bitcast(I32), x_words[0].rearrange("p n r -> p (n r)").bitcast(I32))
        nc.sync.dma_start(w_raw[1][:], w_rows[:, :, H // 2 : H])
        nc.sync.dma_start(e_scale_table[0:16, :].bitcast(I32), e_scales[0].bitcast(I32))
        nc.sync.dma_start(unit_sb[:], unit.rearrange("(p t) o -> p (t o)", t=PACK))
        nc.sync.dma_start(seq_sb[:], seq)
        nc.sync.dma_start(e_table[:].bitcast(I32), e_words[0].rearrange("p n r -> p (n r)").bitcast(I32))

        x_planes = keep.tile([P, S], U8, name="x_planes", align_bytes=64)
        nc.vector.tensor_copy(x_planes[:], x_scale_table[:].indirect(offs_sb[:]))
        x_codes = keep.tile([P, S], U32, name="x_codes", align_bytes=64)
        nc.vector.tensor_copy(x_codes[:], x_table[:].indirect(offs_sb[:]))
        wgt_table = keep.tile([P, W], F32, name="wgt_table", tag="x_then_wgt")
        nc.sync.dma_start(wgt_table[:], wgt)

        w_bf = keep.tile([P, PACK * H], BF16, name="w_bf", align_bytes=64, tag="w_then_e_rows")
        w_dealt = w_bf[:].rearrange("p (t m j) -> p m j t", t=PACK, j=PACK)
        w_src = [w_raw[c][:].rearrange("p j (m t) -> p m j t", t=PACK) for c in range(2)]
        m_half = P // 2
        nc.scalar.copy(w_dealt[:, 0:m_half], w_src[0])
        nc.vector.tensor_copy(w_dealt[:, m_half : m_half + CAST_SPLIT], w_src[1][:, 0:CAST_SPLIT])
        nc.scalar.copy(w_dealt[:, m_half + CAST_SPLIT : P], w_src[1][:, CAST_SPLIT:m_half])

        w_codes = keep.tile([P, H], U32, name="w_codes", align_bytes=64)
        w_planes = keep.tile([P, H], U8, name="w_planes", align_bytes=64)
        y = [psum.tile([P, S], F32, name=f"y{t}") for t in range(PACK)]
        for t in range(PACK):
            cols = slice(t * P, (t + 1) * P)
            nc.vector.quantize_mx(
                out=w_codes[:, cols].bitcast(FP8X4),
                scales=w_planes[:, cols],
                in_=w_bf[:, t * PACK * P : (t + 1) * PACK * P],
            )
            nc.tensor.matmul_mx(
                out=y[t][:],
                lhsT=w_codes[:, cols].bitcast(FP8X4),
                lhsT_scale=w_planes[:, cols],
                rhs=x_codes[:].bitcast(FP8X4),
                rhs_scale=x_planes[:],
                start=True,
                stop=True,
            )

        half_sign = keep.tile([P, PACK], F32, name="half_sign")
        nc.gpsimd.tensor_scalar(half_sign[:], unit_sb[:], 0.0, 0.5, ALU.is_ge, ALU.subtract)
        slope = keep.tile([P, PACK], F32, name="slope")
        nc.gpsimd.tensor_scalar(slope[:], half_sign[:], 2.0 / (0.6 * S), 0.0, ALU.mult, ALU.add)

        e_rows = keep.tile([P, Z], U8, name="e_rows", tag="w_then_e_rows", align_bytes=64)
        nc.vector.tensor_copy(e_rows[:], e_scale_table[:].indirect(plc_sb[:]))
        for q in range(4):
            nc.sync.dma_start(
                e_planes[32 * q : 32 * q + 4, :].bitcast(I32), e_rows[4 * q : 4 * q + 4, :].bitcast(I32)
            )

        agg = keep.tile([P, PACK * V], F32, name="agg")
        fetched = [keep.tile([P, PACK * P], F32, name=f"fetched{h}", tag=f"fetched{h}") for h in range(HALVES)]
        side = Z // 2
        e_codes = []

        def gather_places(b, tag):
            codes = keep.tile([P, side], U32, name=f"e_codes{b}", tag=tag, align_bytes=64)
            nc.vector.tensor_copy(codes[:], e_table[:].indirect(plc_sb[:, b * (side // 16) : (b + 1) * (side // 16)]))
            e_codes.append(codes)

        gather_places(0, "e_codes0")
        for t0 in range(0, PACK, 2):
            ssq = keep.tile([P, 2], F32, name=f"ssq{t0}")
            for u in range(2):
                squares = keep.tile([P, S], F32, name="squares")
                nc.scalar.activation(squares[:], y[t0 + u][:], ACT.Square, accum_out=ssq[:, u : u + 1])
            den = keep.tile([P, 2], F32, name=f"den{t0}")
            nc.vector.scalar_tensor_tensor(den[:], ssq[:], 0.1 * S, slope[:, t0 : t0 + 2], ALU.add, ALU.mult)
            gain = keep.tile([P, 2], F32, name=f"gain{t0}")
            nc.vector.reciprocal(gain[:], den[:])
            signed = []
            for u in range(2):
                t = t0 + u
                mag = keep.tile([P, S], F32, name=f"mag{t}")
                nc.scalar.activation(mag[:], y[t][:], ACT.Abs, scale=unit_sb[:, t : t + 1])
                sg = keep.tile([P, V, 2], F32, name=f"signed{t}", tag=f"signed{t}", align_bytes=64)
                nc.vector.scalar_tensor_tensor(
                    sg[:].rearrange("p v d -> p (v d)"), y[t][:], gain[:, u : u + 1], mag[:], ALU.mult, ALU.mult
                )
                signed.append(sg)
            for u in range(2):
                t = t0 + u
                adder = nc.gpsimd if t0 == 0 else nc.vector
                adder.tensor_tensor(agg[:, t * V : (t + 1) * V], signed[u][:, :, 0], signed[u][:, :, 1], ALU.add)
        for h in range(HALVES):
            for t in range(PACK):
                nc.scalar.activation(
                    fetched[h][:, t * P : (t + 1) * P],
                    agg[:, t * V : (t + 1) * V].indirect(seq_sb[:, h * (P // 16) : (h + 1) * (P // 16)]),
                    ACT.Copy,
                    scale=0.4 / 0.6,
                )

        gather_places(1, f"signed{PACK - 1}")

        sc = [psum.tile([P, Z], F32, name=f"sc{h}") for h in range(HALVES)]
        own = agg[:].rearrange("p (t v) -> p t v", t=PACK)
        for h in range(HALVES):
            hid = keep.tile([P, PACK * P], BF16, name=f"hid{h}", tag=f"hid{h}", align_bytes=64)
            nc.vector.tensor_tensor(
                hid[:].rearrange("p (c i t) -> p c t i", i=4, t=PACK),
                own[:, :, h * P : (h + 1) * P].rearrange("p t (c i) -> p c t i", i=4),
                fetched[h][:].rearrange("p (t c i) -> p c t i", i=4, t=PACK),
                ALU.add,
            )
            hid_codes = keep.tile([P, P], U32, name=f"hid_codes{h}", align_bytes=64)
            hid_planes = keep.tile([P, P], U8, name=f"hid_planes{h}", align_bytes=64)
            nc.vector.quantize_mx(out=hid_codes[:].bitcast(FP8X4), scales=hid_planes[:], in_=hid[:])
            for b in range(2):
                nc.tensor.matmul_mx(
                    out=sc[h][:, b * side : (b + 1) * side],
                    lhsT=hid_codes[:].bitcast(FP8X4),
                    lhsT_scale=hid_planes[:],
                    rhs=e_codes[b][:].bitcast(FP8X4),
                    rhs_scale=e_planes[:, b * side : (b + 1) * side],
                    start=True,
                    stop=True,
                )

        place_wgt = keep.tile([P, Z], F32, name="place_wgt", tag="fetched0")
        nc.scalar.activation(place_wgt[:], wgt_table[:].indirect(plc_sb[:]), ACT.Copy)

        best = [keep.tile([P, 1], F32, name=f"best{h}") for h in range(HALVES)]
        mu = [keep.tile([P, 1], F32, name=f"mu{h}") for h in range(HALVES)]
        for h in range(HALVES):
            nc.vector.tensor_reduce(best[h][:], sc[h][:], AX.X, ALU.max)
            shares = keep.tile([P, Z], F32, name="shares")
            nc.scalar.activation(shares[:], sc[h][:], ACT.Copy, scale=1.0 / Z, accum_out=mu[h][:])
        for h in range(HALVES):
            spread = keep.tile([P, 1], F32, name=f"spread{h}")
            nc.vector.tensor_scalar(spread[:], best[h][:], mu[h][:], 0.3, ALU.subtract, ALU.add)
            centred = keep.tile([P, Z], F32, name=f"centred{h}")
            nc.vector.scalar_tensor_tensor(centred[:], sc[h][:], mu[h][:], place_wgt[:], ALU.subtract, ALU.mult)
            inv = keep.tile([P, 1], F32, name=f"inv{h}")
            nc.vector.reciprocal(inv[:], spread[:])
            rows = slice(h * P, (h + 1) * P)
            if h == 0:
                res = keep.tile([P, Z], F32, name="res")
                nc.scalar.activation(res[:], centred[:], ACT.Copy, scale=inv[:])
                nc.sync.dma_start(out[rows, :], res[:])
            else:
                left = keep.tile([P, LAST_SPLIT], F32, name="left")
                right = keep.tile([P, Z - LAST_SPLIT], F32, name="right")
                nc.scalar.activation(left[:], centred[:, 0:LAST_SPLIT], ACT.Copy, scale=inv[:])
                nc.vector.tensor_scalar(right[:], centred[:, LAST_SPLIT:Z], inv[:], None, ALU.mult)
                nc.scalar.dma_start(out[rows, 0:LAST_SPLIT], left[:])
                nc.sync.dma_start(out[rows, LAST_SPLIT:Z], right[:])
